import numpy as np
import ml_dtypes


def mxq(x, axis, fmt="e4m3"):
    dtype, down = {"e4m3": (ml_dtypes.float8_e4m3fn, 7), "e5m2": (ml_dtypes.float8_e5m2, 14)}[fmt]
    v = np.moveaxis(np.asarray(x, np.float32).astype(ml_dtypes.bfloat16).astype(np.float64), axis, -1)
    blocks = v.reshape(v.shape[:-1] + (-1, 32))
    amax = np.abs(blocks).max(-1, keepdims=True)
    byte = np.maximum(np.where(amax > 0, np.frexp(amax)[1] - 1 + 127, 0) - down, 1)
    scale = np.exp2(byte - 127.0)
    codes = (blocks / scale).astype(np.float32).astype(dtype).astype(np.float64)
    return np.moveaxis((codes * scale).reshape(v.shape), -1, axis)


WIDE = False


def mx_kscale(k):
    if not WIDE:
        return np.ones(k)
    levels = np.array([10, -10, 5, -5, 0])
    if k % 512:
        return np.exp2(np.random.permutation(np.resize(levels, k // 32))).repeat(32)
    a = np.empty((k // 512, 16))
    for p in range(k // 512):
        a[p, :8] = np.random.permutation(np.resize(levels, 8))
        for g in range(8):
            far = levels[np.abs(levels - a[p, g]) >= 10]
            a[p, g + 8] = far[np.random.randint(len(far))]
    return np.exp2(a.ravel()).repeat(32)


def f64(x):
    return np.asarray(x).astype(np.float64)


def striped(idx):
    return np.tile(idx.reshape(-1, 16).T, (8, 1)).astype(np.uint16)


def unstriped(offs):
    return offs[:16].T.reshape(-1).astype(np.int64)


def striped8(idx):
    return np.concatenate([x.reshape(-1, 16).T for x in idx]).astype(np.uint16)


def runs(offs, k):
    lists = np.stack([offs[16 * r : 16 * r + 16].T.reshape(-1) for r in range(8)]).astype(np.int64)
    return lists[np.arange(k) % 512 // 64]


def pack_weight(w):
    k, n = w.shape
    w = f64(np.asarray(w, np.float32).astype(ml_dtypes.bfloat16)).reshape(k // 32, 32, n)
    amax = np.abs(w).max(1)
    byte = np.clip(np.where(amax > 0, np.frexp(amax)[1] - 1 + 127 - 7, 1), 1, 254)
    scaled = (w * np.exp2(127.0 - byte)[:, None, :]).reshape(k, n).astype(np.float32)
    words = np.ascontiguousarray(scaled.reshape(k // 512, 128, 4, n).transpose(0, 1, 3, 2)).astype(ml_dtypes.float8_e4m3fn).view(np.uint8)
    return words, np.ascontiguousarray(byte.astype(np.uint8).reshape(k // 512, 16, n))


def unpack_weight(words, scales):
    g, p, n, _ = words.shape
    vals = np.ascontiguousarray(words).view(ml_dtypes.float8_e4m3fn).astype(np.float64) * np.repeat(np.exp2(scales.astype(np.float64) - 127.0), 8, axis=1)[..., None]
    return vals.transpose(0, 1, 3, 2).reshape(g * 512, n)


E2M1 = np.array([0.0, 0.5, 1.0, 1.5, 2.0, 3.0, 4.0, 6.0, -0.0, -0.5, -1.0, -1.5, -2.0, -3.0, -4.0, -6.0])


def pack_fp4(w):
    k, n = w.shape
    w = f64(np.asarray(w, np.float32).astype(ml_dtypes.bfloat16)).reshape(k // 32, 32, n)
    amax = np.abs(w).max(1)
    mant, ex = np.frexp(amax / 6.0)
    byte = np.clip(np.where(amax > 0, np.where(mant > 0.5, ex, ex - 1) + 127, 1), 1, 254)
    scaled = (w * np.exp2(127.0 - byte)[:, None, :]).reshape(k, n).astype(np.float32)
    c = np.ascontiguousarray(scaled.reshape(k // 512, 128, 4, n).transpose(0, 1, 3, 2)).astype(ml_dtypes.float4_e2m1fn).view(np.uint8) & 0xF
    words = (c[..., 0::2] | (c[..., 1::2] << 4)).reshape(k // 512, 128, 2 * n)
    return np.ascontiguousarray(words), np.ascontiguousarray(byte.astype(np.uint8).reshape(k // 512, 16, n))


def unpack_fp4(words, scales):
    g, _, n = scales.shape
    words = np.ascontiguousarray(words).reshape(g, 128, n, 2)
    nib = np.empty((g, 128, n, 4), np.uint8)
    nib[..., 0::2] = words & 0xF
    nib[..., 1::2] = words >> 4
    vals = E2M1[nib] * np.repeat(np.exp2(scales.astype(np.float64) - 127.0), 8, axis=1)[..., None]
    return vals.transpose(0, 1, 3, 2).reshape(g * 512, n)


def sigmoid(v):
    return 1.0 / (1.0 + np.exp(-np.maximum(v, -700.0)))

def planes(y):
    n, m = y.shape
    v = y.astype(np.float32).astype(ml_dtypes.bfloat16).astype(np.float64).reshape(n // 32, 32, m)
    top = np.abs(v).max(1)
    byte = np.clip(np.where(top > 0, np.frexp(top)[1] - 1 + 127 - 7, 1), 1, 254)
    codes = (v * np.exp2(127.0 - byte)[:, None, :]).reshape(n, m).astype(np.float32).astype(ml_dtypes.float8_e4m3fn).view(np.uint8)
    words = codes.reshape(n // 512, 128, 4, m).transpose(0, 1, 3, 2)
    return np.ascontiguousarray(words), np.ascontiguousarray(byte.astype(np.uint8).reshape(n // 512, 16, m))


K, T, S, N, G, H, W = 512, 2048, 512, 512, 2048, 512, 384


def setup_inputs():
    n = np.random.standard_normal
    s = mx_kscale(K)[:, None]
    u = mx_kscale(S)
    packed_xT = pack_weight(n((K, T)) * s)
    packed_dT = pack_weight(n((K, G)) / s)
    packed_w1 = pack_fp4(n((H, N)) / np.sqrt(H) / u[:, None])
    return {
        "x_words": packed_xT[0],
        "x_scales": packed_xT[1],
        "d_words": packed_dT[0],
        "d_scales": packed_dT[1],
        "gn": (np.random.uniform(0.5, 1.5, (H, 1)) * u[:, None]).astype(np.float32),
        "w1_words": packed_w1[0],
        "w1_scales": packed_w1[1],
        "sl": np.random.uniform(1.0, 2.0, (N, 1)).astype(np.float32),
        "th": (0.5 * n((N, 1))).astype(np.float32),
        "offs": striped(np.random.permutation(T)[:S]),
        "k1": striped8(np.random.randint(0, G, (8, H))),
        "n1": striped(np.random.permutation(S)[:W]),
        "n2": striped(np.random.permutation(S)[:W]),
        "n3": striped(np.random.permutation(S)),
        "n4": striped(np.random.permutation(S)),
    }


def reference(x_words, x_scales, d_words, d_scales, gn, w1_words, w1_scales, sl, th, offs, k1, n1, n2, n3, n4):
    d_k1 = unpack_weight(d_words, d_scales)[np.arange(K)[:, None], runs(k1, K)]
    xq = unpack_weight(x_words, x_scales)[:, unstriped(offs)]
    h = 0.0625 * (d_k1.T @ xq)
    old = h[:, unstriped(n1)]
    pa = h[:, unstriped(n2)]
    ra = old / (np.abs(pa) + 0.5)
    ds = h.copy()
    ds[:, unstriped(n1)] = ra
    z = f64(gn) * ds
    h2 = unpack_fp4(w1_words, w1_scales).T @ mxq(z, 0, "e4m3")
    st = h2 - h2[:, unstriped(n3)]
    sg = sigmoid(f64(sl) * (st[:, unstriped(n4)] - f64(th)))
    out_0 = h2 * sg
    return (out_0,) + planes(out_0)

@@ -1,0 +1,214 @@
+from contextlib import ExitStack
+
+import concourse.mybir as mybir
+
+K, T, S, N, G, H, W = 512, 2048, 512, 512, 2048, 512, 384
+FLOPS = 2 * K * H * S + 2 * H * N * S
+
+F32 = mybir.dt.float32
+BF16 = mybir.dt.bfloat16
+I32 = mybir.dt.int32
+U32 = mybir.dt.uint32
+U16 = mybir.dt.uint16
+U8 = mybir.dt.uint8
+FP8X4 = mybir.dt.float8_e4m3fn_x4
+FP4X4 = mybir.dt.float4_e2m1fn_x4
+ALU = mybir.AluOpType
+ACT = mybir.ActivationFunctionType
+
+P = 128
+PACK = 4
+HALF = S // 2
+
+
+def tile_picked_pqlayknormehq_none_po_kernel(
+    tc, x_words, x_scales, d_words, d_scales, gn, w1_words, w1_scales, sl, th, offs, k1, n1, n2, n3, n4, out_0, out_1, out_2
+):
+    nc = tc.nc
+    with ExitStack() as ctx:
+        keep = ctx.enter_context(tc.tile_pool(name="keep", bufs=1))
+        psum = ctx.enter_context(tc.psum_pool(name="psum", bufs=1))
+
+        def tile(name, width, dtype):
+            return keep.tile([P, width], dtype, name=name, align_bytes=64)
+
+        def load_list(name, src):
+            lst = keep.tile([P, src.shape[1]], U16, name=name)
+            nc.sync.dma_start(lst[:], src)
+            return lst
+
+        def load_scale_rows(queue, plane, rows):
+            for q in range(4):
+                queue.dma_start(plane[32 * q : 32 * q + 4, :].bitcast(I32), rows[4 * q : 4 * q + 4, :].bitcast(I32))
+
+        def load_column(name, src):
+            col = tile(name, PACK, F32)
+            nc.gpsimd.dma_start(col[:], src.rearrange("(p t) o -> p (t o)", t=PACK))
+            return col
+
+        d_scale_tab = tile("d_scale_tab", G, U8)
+        x_scale_tab = tile("x_scale_tab", T, U8)
+        w_scale_raw = tile("w_scale_raw", N, U8)
+        nc.gpsimd.memset(d_scale_tab[:].bitcast(I32), 0)
+        nc.vector.memset(x_scale_tab[:].bitcast(I32), 0)
+        nc.vector.memset(w_scale_raw[:].bitcast(I32), 0)
+
+        k1_t = load_list("k1_t", k1)
+        d_word_tab = tile("d_word_tab", G, I32)
+        nc.sync.dma_start(d_word_tab[:], d_words[0].rearrange("p n t -> p (n t)").bitcast(I32))
+        offs_t = load_list("offs_t", offs)
+        for b in range(2):
+            nc.scalar.dma_start(d_scale_tab[b:P:16, :].bitcast(I32), d_scales[0][b:16:2, :].bitcast(I32))
+        n2_t = load_list("n2_t", n2)
+        x_word_tab = tile("x_word_tab", T, I32)
+        nc.sync.dma_start(x_word_tab[:], x_words[0].rearrange("p n t -> p (n t)").bitcast(I32))
+        load_scale_rows(nc.gpsimd, x_scale_tab, x_scales[0])
+        n1_t = load_list("n1_t", n1)
+        n3_t = load_list("n3_t", n3)
+        n4_t = load_list("n4_t", n4)
+        w_word_raw = tile("w_word_raw", 2 * N, U8)
+        nc.gpsimd.dma_start(w_word_raw[:].bitcast(I32), w1_words[0].bitcast(I32))
+        gn_c = load_column("gn_c", gn)
+        load_scale_rows(nc.gpsimd, w_scale_raw, w1_scales[0])
+        sl_c = load_column("sl_c", sl)
+        th_c = load_column("th_c", th)
+
+        d_scale_got = tile("d_scale_got", H, U8)
+        nc.vector.tensor_copy(d_scale_got[:], d_scale_tab[:].indirect(k1_t[:]))
+        d_scale = tile("d_scale", H, U8)
+        nc.vector.tensor_copy(
+            d_scale[:].rearrange("p (t m) -> p t m", t=PACK), d_scale_got[:].rearrange("p (m t) -> p t m", t=PACK)
+        )
+        for b in range(2):
+            nc.scalar.dma_start(d_scale[2 + b : P : 32, :].bitcast(I32), d_scale[16 + b : P : 32, :].bitcast(I32))
+        d_word_got = tile("d_word_got", H, I32)
+        nc.vector.tensor_copy(d_word_got[:].bitcast(U32), d_word_tab[:].bitcast(U32).indirect(k1_t[:]))
+        d_word = tile("d_word", H, I32)
+        nc.vector.tensor_copy(
+            d_word[:].rearrange("p (t m) -> p t m", t=PACK), d_word_got[:].rearrange("p (m t) -> p t m", t=PACK)
+        )
+        x_scale = tile("x_scale", S, U8)
+        nc.vector.tensor_copy(x_scale[:], x_scale_tab[:].indirect(offs_t[:]))
+        x_word = tile("x_word", S, I32)
+        nc.vector.tensor_copy(x_word[:].bitcast(U32), x_word_tab[:].bitcast(U32).indirect(offs_t[:]))
+
+        w_word = tile("w_word", 2 * N, U8)
+        nc.scalar.copy(
+            w_word[:].bitcast(U16).rearrange("p (t m) -> p t m", t=PACK),
+            w_word_raw[:].bitcast(U16).rearrange("p (m t) -> p t m", t=PACK),
+        )
+        w_scale = tile("w_scale", N, U8)
+        nc.gpsimd.tensor_copy(
+            w_scale[:].rearrange("p (t m) -> p t m", t=PACK), w_scale_raw[:].rearrange("p (m t) -> p t m", t=PACK)
+        )
+        bias_c = tile("bias_c", PACK, F32)
+        sl_th = tile("sl_th", PACK, F32)
+        nc.gpsimd.tensor_tensor(sl_th[:], sl_c[:], th_c[:], ALU.mult)
+        nc.gpsimd.tensor_scalar(bias_c[:], sl_th[:], -1.0, 0.0, ALU.mult, ALU.add)
+
+        h_ps = [psum.tile([P, S], F32, name=f"h_ps{t}") for t in range(PACK)]
+        for t in range(PACK):
+            cols = slice(P * t, P * (t + 1))
+            nc.tensor.matmul_mx(
+                h_ps[t][:], lhsT=d_word[:, cols].bitcast(FP8X4), lhsT_scale=d_scale[:, cols],
+                rhs=x_word[:].bitcast(FP8X4), rhs_scale=x_scale[:], start=True, stop=True,
+            )
+
+        ds = [tile(f"ds{t}", S, F32) for t in range(PACK)]
+        mag = [tile(f"mag{t}", W, F32) for t in range(PACK)]
+        root = [tile(f"root{t}", W, F32) for t in range(PACK)]
+        inv = [tile(f"inv{t}", W, F32) for t in range(2)]
+        z_rows = keep.tile([P, PACK, S], BF16, name="z_rows", align_bytes=64)
+
+        def shared(name, tag):
+            return keep.tile([P, W], F32, name=name, tag=tag, align_bytes=64)
+
+        for t in range(PACK):
+            nc.scalar.activation(ds[t][:], h_ps[t][:], ACT.Copy, scale=0.0625)
+        pa = [shared(f"pa{t}", f"pa{t}") for t in range(PACK)]
+        for t in range(PACK):
+            nc.vector.tensor_copy(pa[t][:], ds[t][:].indirect(n2_t[:]))
+        old = [shared(f"old{t}", f"old{t}") for t in range(2)]
+        for t in range(2):
+            nc.vector.tensor_copy(old[t][:], ds[t][:].indirect(n1_t[:]))
+        for t in range(PACK):
+            nc.scalar.activation(mag[t][:], pa[t][:], ACT.Abs)
+            nc.scalar.activation(root[t][:], mag[t][:], ACT.Abs_reciprocal_sqrt, bias=0.5)
+            if t < 2:
+                nc.scalar.activation(inv[t][:], root[t][:], ACT.Square)
+        ra = [shared(f"ra{t}", f"pa{t + 2}") for t in range(2)]
+        for t in range(2):
+            nc.vector.tensor_tensor(ra[t][:], old[t][:], inv[t][:], ALU.mult)
+        for t in range(2):
+            nc.scalar.activation(ds[t][:].indirect(n1_t[:]), ra[t][:], ACT.Copy)
+        for t in range(2, PACK):
+            part = shared(f"part{t}", f"old{t - 2}")
+            nc.vector.tensor_tensor(part[:], ds[t][:].indirect(n1_t[:]), root[t][:], ALU.mult)
+            nc.vector.tensor_tensor(ds[t][:].indirect(n1_t[:]), part[:], root[t][:], ALU.mult)
+        for t in range(3):
+            nc.scalar.activation(z_rows[:, t, :], ds[t][:], ACT.Copy, scale=gn_c[:, t : t + 1])
+        nc.vector.tensor_scalar(z_rows[:, 3, :], ds[3][:], gn_c[:, 3:4], None, ALU.mult)
+
+        h2_ps = [psum.tile([P, S], F32, name=f"h2_ps{t}") for t in range(PACK)]
+        z_in = [keep.tile([P, HALF, PACK], BF16, name=f"z_in{u}", align_bytes=64) for u in range(2)]
+        z_word = [tile(f"z_word{u}", HALF, U32) for u in range(2)]
+        z_scale = [tile(f"z_scale{u}", HALF, U8) for u in range(2)]
+        for u in range(2):
+            nc.gpsimd.memset(z_scale[u][:].bitcast(I32), 0)
+        for u in range(2):
+            cols = slice(HALF * u, HALF * (u + 1))
+            nc.vector.tensor_copy(z_in[u][:], z_rows[:, :, cols].rearrange("p t c -> p c t"))
+        for u in range(2):
+            nc.vector.quantize_mx(z_word[u][:].bitcast(FP8X4), z_scale[u][:], z_in[u][:].rearrange("p c t -> p (c t)"))
+        for u in range(2):
+            cols = slice(HALF * u, HALF * (u + 1))
+            for t in range(PACK):
+                nc.tensor.matmul_mx(
+                    h2_ps[t][:, cols], lhsT=w_word[:, 2 * P * t : 2 * P * (t + 1)].bitcast(FP4X4),
+                    lhsT_scale=w_scale[:, P * t : P * (t + 1)],
+                    rhs=z_word[u][:].bitcast(FP8X4), rhs_scale=z_scale[u][:], start=True, stop=True,
+                )
+
+        h2 = [tile(f"h2_{t}", S, F32) for t in range(PACK)]
+        far = [tile(f"far{t}", S, F32) for t in range(PACK)]
+        st = [tile(f"st{t}", S, F32) for t in range(PACK)]
+        sg = [tile(f"sg{t}", S, F32) for t in range(PACK)]
+        y = [keep.tile([P, PACK, HALF], F32, name=f"y{u}", align_bytes=64) for u in range(2)]
+        y_in = [keep.tile([P, HALF, PACK], BF16, name=f"y_in{u}", align_bytes=64) for u in range(2)]
+        y_word = [tile(f"y_word{u}", HALF, I32) for u in range(2)]
+        y_scale = [tile(f"y_scale{u}", HALF, U8) for u in range(2)]
+        out_rows = out_0.rearrange("(p t) c -> p t c", t=PACK)
+        out_words = out_1[0].rearrange("p n t -> p (n t)").bitcast(I32)
+        LC = HALF // 16
+        halves = [(slice(HALF * u, HALF * (u + 1)), slice(LC * u, LC * (u + 1))) for u in range(2)]
+        nc.vector.tensor_copy(h2[0][:], h2_ps[0][:])
+        for t in range(1, PACK):
+            nc.scalar.copy(h2[t][:], h2_ps[t][:])
+        for t in range(PACK):
+            for cols, part_list in halves:
+                if t != 1:
+                    nc.vector.tensor_copy(far[t][:, cols], h2[t][:].indirect(n3_t[:, part_list]))
+                else:
+                    nc.scalar.activation(far[t][:, cols], h2[t][:].indirect(n3_t[:, part_list]), ACT.Copy)
+            nc.vector.tensor_tensor(st[t][:], h2_ps[t][:], far[t][:], ALU.subtract)
+        for t in range(PACK):
+            for cols, part_list in halves:
+                nc.scalar.activation(
+                    sg[t][:, cols], st[t][:].indirect(n4_t[:, part_list]), ACT.Sigmoid,
+                    bias=bias_c[:, t : t + 1], scale=sl_c[:, t : t + 1],
+                )
+        for t in range(PACK):
+            for u in range(2):
+                cols = halves[u][0]
+                nc.vector.tensor_tensor(y[u][:, t, :], h2_ps[t][:, cols], sg[t][:, cols], ALU.mult)
+                nc.sync.dma_start(out_rows[:, t, cols], y[u][:, t, :])
+        for u in range(2):
+            cols = slice(HALF * u, HALF * (u + 1))
+            nc.vector.tensor_copy(y_in[u][:], y[u][:].rearrange("p t c -> p c t"))
+            nc.vector.quantize_mx(y_word[u][:].bitcast(FP8X4), y_scale[u][:], y_in[u][:].rearrange("p c t -> p (c t)"))
+            nc.sync.dma_start(out_words[:, cols], y_word[u][:])
+            for q in range(4):
+                queue = nc.sync if q % 2 == 0 else nc.scalar
+                queue.dma_start(
+                    out_2[0][4 * q : 4 * q + 4, cols].bitcast(I32), y_scale[u][32 * q : 32 * q + 4, :].bitcast(I32)
+                )

@@ -41,53 +41,49 @@ def tile_picked_pqlayknormehq_none_po_kernel(
             for q in range(4):
                 queue.dma_start(plane[32 * q : 32 * q + 4, :].bitcast(I32), rows[4 * q : 4 * q + 4, :].bitcast(I32))
 
-        def load_column(name, src):
-            col = tile(name, PACK, F32)
-            nc.gpsimd.dma_start(col[:], src.rearrange("(p t) o -> p (t o)", t=PACK))
-            return col
-
-        d_scale_tab = tile("d_scale_tab", G, U8)
-        x_scale_tab = tile("x_scale_tab", T, U8)
-        w_scale_raw = tile("w_scale_raw", N, U8)
-        nc.gpsimd.memset(d_scale_tab[:].bitcast(I32), 0)
-        nc.vector.memset(x_scale_tab[:].bitcast(I32), 0)
-        nc.vector.memset(w_scale_raw[:].bitcast(I32), 0)
-
+        d_scale_tab = keep.tile([P, G], U8, name="d_scale_tab", tag="early", align_bytes=64)
+        nc.sync.dma_start(
+            d_scale_tab[:].bitcast(I32),
+            d_scales[0].bitcast(I32).unsqueeze(1).to_broadcast([16, 8, G // 4]),
+        )
         k1_t = load_list("k1_t", k1)
-        d_word_tab = tile("d_word_tab", G, I32)
-        nc.sync.dma_start(d_word_tab[:], d_words[0].rearrange("p n t -> p (n t)").bitcast(I32))
         offs_t = load_list("offs_t", offs)
-        for b in range(2):
-            nc.scalar.dma_start(d_scale_tab[b:P:16, :].bitcast(I32), d_scales[0][b:16:2, :].bitcast(I32))
         n2_t = load_list("n2_t", n2)
-        x_word_tab = tile("x_word_tab", T, I32)
-        nc.sync.dma_start(x_word_tab[:], x_words[0].rearrange("p n t -> p (n t)").bitcast(I32))
-        load_scale_rows(nc.gpsimd, x_scale_tab, x_scales[0])
+        d_word_tab = keep.tile([P, G], I32, name="d_word_tab", tag="d_words", align_bytes=64)
+        nc.sync.dma_start(d_word_tab[:], d_words[0].rearrange("p n t -> p (n t)").bitcast(I32))
         n1_t = load_list("n1_t", n1)
         n3_t = load_list("n3_t", n3)
         n4_t = load_list("n4_t", n4)
-        w_word_raw = tile("w_word_raw", 2 * N, U8)
-        nc.gpsimd.dma_start(w_word_raw[:].bitcast(I32), w1_words[0].bitcast(I32))
-        gn_c = load_column("gn_c", gn)
-        load_scale_rows(nc.gpsimd, w_scale_raw, w1_scales[0])
-        sl_c = load_column("sl_c", sl)
-        th_c = load_column("th_c", th)
+        x_word_tab = keep.tile([P, T], I32, name="x_word_tab", tag="x_words", align_bytes=64)
+        nc.sync.dma_start(x_word_tab[:], x_words[0].rearrange("p n t -> p (n t)").bitcast(I32))
+        x_scale_tab = tile("x_scale_tab", T, U8)
+        nc.gpsimd.memset(x_scale_tab[:].bitcast(I32), 0)
+        load_scale_rows(nc.gpsimd, x_scale_tab, x_scales[0])
 
-        d_scale_got = tile("d_scale_got", H, U8)
+        d_scale_got = keep.tile([P, H], U8, name="d_scale_got", tag="scale_stage", align_bytes=64)
         nc.vector.tensor_copy(d_scale_got[:], d_scale_tab[:].indirect(k1_t[:]))
+        w_word_raw = keep.tile([P, 2 * N], U8, name="w_word_raw", tag="early", align_bytes=64)
+        nc.gpsimd.dma_start(w_word_raw[:].bitcast(I32), w1_words[0].bitcast(I32))
         d_scale = tile("d_scale", H, U8)
         nc.vector.tensor_copy(
             d_scale[:].rearrange("p (t m) -> p t m", t=PACK), d_scale_got[:].rearrange("p (m t) -> p t m", t=PACK)
         )
-        for b in range(2):
-            nc.scalar.dma_start(d_scale[2 + b : P : 32, :].bitcast(I32), d_scale[16 + b : P : 32, :].bitcast(I32))
-        d_word_got = tile("d_word_got", H, I32)
+        for r in range(1, 4):
+            nc.scalar.dma_start(d_scale[r:P:32, :].bitcast(I32), d_scale[8 * r : P : 32, :].bitcast(I32))
+        w_scale_raw = keep.tile([P, N], U8, name="w_scale_raw", tag="scale_stage", align_bytes=64)
+        nc.vector.memset(w_scale_raw[:].bitcast(I32), 0)
+        load_scale_rows(nc.scalar, w_scale_raw, w1_scales[0])
+        d_word_got = keep.tile([P, H], I32, name="d_word_got", tag="word_stage", align_bytes=64)
         nc.vector.tensor_copy(d_word_got[:].bitcast(U32), d_word_tab[:].bitcast(U32).indirect(k1_t[:]))
         d_word = tile("d_word", H, I32)
         nc.vector.tensor_copy(
             d_word[:].rearrange("p (t m) -> p t m", t=PACK), d_word_got[:].rearrange("p (m t) -> p t m", t=PACK)
         )
-        x_scale = tile("x_scale", S, U8)
+        per_row = keep.tile([P, 3, 8], F32, name="per_row", tag="word_stage", align_bytes=64)
+        for slot, src in enumerate((gn, sl, th)):
+            nc.gpsimd.dma_start(per_row[:, slot, 0:PACK], src.rearrange("(p t) o -> p (t o)", t=PACK))
+        gn_c, sl_c, th_c = (per_row[:, slot, :] for slot in range(3))
+        x_scale = keep.tile([P, S], U8, name="x_scale", tag="d_words", align_bytes=64)
         nc.vector.tensor_copy(x_scale[:], x_scale_tab[:].indirect(offs_t[:]))
         x_word = tile("x_word", S, I32)
         nc.vector.tensor_copy(x_word[:].bitcast(U32), x_word_tab[:].bitcast(U32).indirect(offs_t[:]))
@@ -97,16 +93,16 @@ def tile_picked_pqlayknormehq_none_po_kernel(
             w_word[:].bitcast(U16).rearrange("p (t m) -> p t m", t=PACK),
             w_word_raw[:].bitcast(U16).rearrange("p (m t) -> p t m", t=PACK),
         )
-        w_scale = tile("w_scale", N, U8)
-        nc.gpsimd.tensor_copy(
+        w_scale = keep.tile([P, N], U8, name="w_scale", tag="x_words", align_bytes=64)
+        nc.vector.tensor_copy(
             w_scale[:].rearrange("p (t m) -> p t m", t=PACK), w_scale_raw[:].rearrange("p (m t) -> p t m", t=PACK)
         )
         bias_c = tile("bias_c", PACK, F32)
         sl_th = tile("sl_th", PACK, F32)
-        nc.gpsimd.tensor_tensor(sl_th[:], sl_c[:], th_c[:], ALU.mult)
+        nc.gpsimd.tensor_tensor(sl_th[:], sl_c[:, 0:PACK], th_c[:, 0:PACK], ALU.mult)
         nc.gpsimd.tensor_scalar(bias_c[:], sl_th[:], -1.0, 0.0, ALU.mult, ALU.add)
 
-        h_ps = [psum.tile([P, S], F32, name=f"h_ps{t}") for t in range(PACK)]
+        h_ps = [psum.tile([P, S], F32, name=f"h_ps{t}", tag=f"bank{t}") for t in range(PACK)]
         for t in range(PACK):
             cols = slice(P * t, P * (t + 1))
             nc.tensor.matmul_mx(
@@ -114,42 +110,52 @@ def tile_picked_pqlayknormehq_none_po_kernel(
                 rhs=x_word[:].bitcast(FP8X4), rhs_scale=x_scale[:], start=True, stop=True,
             )
 
-        ds = [tile(f"ds{t}", S, F32) for t in range(PACK)]
-        mag = [tile(f"mag{t}", W, F32) for t in range(PACK)]
-        root = [tile(f"root{t}", W, F32) for t in range(PACK)]
-        inv = [tile(f"inv{t}", W, F32) for t in range(2)]
-        z_rows = keep.tile([P, PACK, S], BF16, name="z_rows", align_bytes=64)
+        def work(name, tag=None):
+            return keep.tile([P, W], F32, name=name, tag=tag or name, align_bytes=64)
 
-        def shared(name, tag):
-            return keep.tile([P, W], F32, name=name, tag=tag, align_bytes=64)
+        ds = [tile(f"ds{t}", S, F32) for t in range(PACK)]
+        pa = [work(f"pa{t}") for t in range(PACK)]
+        mag = [keep.tile([P, W], F32, name=f"mag{t}", tag=f"mag{t}", align_bytes=64) for t in range(PACK)]
+        root = [work(f"root{t}") for t in range(PACK)]
+        inv = [work(f"inv{t}") for t in range(2)]
+        old = [work(f"old{t}") for t in range(PACK)]
+        z_rows = keep.tile([P, PACK, S], BF16, name="z_rows", align_bytes=64)
 
         for t in range(PACK):
             nc.scalar.activation(ds[t][:], h_ps[t][:], ACT.Copy, scale=0.0625)
-        pa = [shared(f"pa{t}", f"pa{t}") for t in range(PACK)]
         for t in range(PACK):
             nc.vector.tensor_copy(pa[t][:], ds[t][:].indirect(n2_t[:]))
-        old = [shared(f"old{t}", f"old{t}") for t in range(2)]
-        for t in range(2):
-            nc.vector.tensor_copy(old[t][:], ds[t][:].indirect(n1_t[:]))
+        for t in range(PACK):
+            if t == 1:
+                nc.scalar.activation(old[t][:], ds[t][:].indirect(n1_t[:]), ACT.Copy)
+            else:
+                nc.vector.tensor_copy(old[t][:], ds[t][:].indirect(n1_t[:]))
         for t in range(PACK):
             nc.scalar.activation(mag[t][:], pa[t][:], ACT.Abs)
             nc.scalar.activation(root[t][:], mag[t][:], ACT.Abs_reciprocal_sqrt, bias=0.5)
             if t < 2:
                 nc.scalar.activation(inv[t][:], root[t][:], ACT.Square)
-        ra = [shared(f"ra{t}", f"pa{t + 2}") for t in range(2)]
+        ra = keep.tile([P, 2, W], F32, name="ra", tag="mag2", align_bytes=64)
         for t in range(2):
-            nc.vector.tensor_tensor(ra[t][:], old[t][:], inv[t][:], ALU.mult)
-        for t in range(2):
-            nc.scalar.activation(ds[t][:].indirect(n1_t[:]), ra[t][:], ACT.Copy)
+            nc.vector.tensor_tensor(ra[:, t, :], old[t][:], inv[t][:], ALU.mult)
+        part = {2: work("part2", "old1"), 3: work("part3", "inv1")}
         for t in range(2, PACK):
-            part = shared(f"part{t}", f"old{t - 2}")
-            nc.vector.tensor_tensor(part[:], ds[t][:].indirect(n1_t[:]), root[t][:], ALU.mult)
-            nc.vector.tensor_tensor(ds[t][:].indirect(n1_t[:]), part[:], root[t][:], ALU.mult)
-        for t in range(3):
+            nc.vector.tensor_tensor(part[t][:], old[t][:], root[t][:], ALU.mult)
+        for t in range(2):
+            nc.scalar.activation(ds[t][:].indirect(n1_t[:]), ra[:, t, :], ACT.Copy)
+        for t in range(2, PACK):
+            nc.vector.tensor_tensor(ds[t][:].indirect(n1_t[:]), part[t][:], root[t][:], ALU.mult)
+        for t in range(2):
             nc.scalar.activation(z_rows[:, t, :], ds[t][:], ACT.Copy, scale=gn_c[:, t : t + 1])
-        nc.vector.tensor_scalar(z_rows[:, 3, :], ds[3][:], gn_c[:, 3:4], None, ALU.mult)
+        for t in range(2, PACK):
+            for u in range(2):
+                cols = slice(HALF * u, HALF * (u + 1))
+                nc.vector.tensor_scalar(z_rows[:, t, cols], ds[t][:, cols], gn_c[:, t : t + 1], None, ALU.mult)
 
-        h2_ps = [psum.tile([P, S], F32, name=f"h2_ps{t}") for t in range(PACK)]
+        h2_ps = [
+            [psum.tile([P, HALF], F32, name=f"h2_ps{u}{t}", tag=f"bank{PACK * (1 - u) + t}") for t in range(PACK)]
+            for u in range(2)
+        ]
         z_in = [keep.tile([P, HALF, PACK], BF16, name=f"z_in{u}", align_bytes=64) for u in range(2)]
         z_word = [tile(f"z_word{u}", HALF, U32) for u in range(2)]
         z_scale = [tile(f"z_scale{u}", HALF, U8) for u in range(2)]
@@ -157,23 +163,24 @@ def tile_picked_pqlayknormehq_none_po_kernel(
             nc.gpsimd.memset(z_scale[u][:].bitcast(I32), 0)
         for u in range(2):
             cols = slice(HALF * u, HALF * (u + 1))
-            nc.vector.tensor_copy(z_in[u][:], z_rows[:, :, cols].rearrange("p t c -> p c t"))
+            nc.vector.tensor_copy(
+                z_in[u][:].rearrange("p (c i) t -> p c t i", i=4), z_rows[:, :, cols].rearrange("p t (c i) -> p c t i", i=4)
+            )
         for u in range(2):
             nc.vector.quantize_mx(z_word[u][:].bitcast(FP8X4), z_scale[u][:], z_in[u][:].rearrange("p c t -> p (c t)"))
         for u in range(2):
             cols = slice(HALF * u, HALF * (u + 1))
             for t in range(PACK):
                 nc.tensor.matmul_mx(
-                    h2_ps[t][:, cols], lhsT=w_word[:, 2 * P * t : 2 * P * (t + 1)].bitcast(FP4X4),
+                    h2_ps[u][t][:], lhsT=w_word[:, 2 * P * t : 2 * P * (t + 1)].bitcast(FP4X4),
                     lhsT_scale=w_scale[:, P * t : P * (t + 1)],
                     rhs=z_word[u][:].bitcast(FP8X4), rhs_scale=z_scale[u][:], start=True, stop=True,
                 )
 
         h2 = [tile(f"h2_{t}", S, F32) for t in range(PACK)]
-        far = [tile(f"far{t}", S, F32) for t in range(PACK)]
+        far = [keep.tile([P, S], F32, name=f"far{t}", tag=f"far{t}", align_bytes=64) for t in range(PACK)]
         st = [tile(f"st{t}", S, F32) for t in range(PACK)]
         sg = [tile(f"sg{t}", S, F32) for t in range(PACK)]
-        y = [keep.tile([P, PACK, HALF], F32, name=f"y{u}", align_bytes=64) for u in range(2)]
         y_in = [keep.tile([P, HALF, PACK], BF16, name=f"y_in{u}", align_bytes=64) for u in range(2)]
         y_word = [tile(f"y_word{u}", HALF, I32) for u in range(2)]
         y_scale = [tile(f"y_scale{u}", HALF, U8) for u in range(2)]
@@ -181,30 +188,40 @@ def tile_picked_pqlayknormehq_none_po_kernel(
         out_words = out_1[0].rearrange("p n t -> p (n t)").bitcast(I32)
         LC = HALF // 16
         halves = [(slice(HALF * u, HALF * (u + 1)), slice(LC * u, LC * (u + 1))) for u in range(2)]
-        nc.vector.tensor_copy(h2[0][:], h2_ps[0][:])
-        for t in range(1, PACK):
-            nc.scalar.copy(h2[t][:], h2_ps[t][:])
+        for u in range(2):
+            for t in range(PACK):
+                nc.scalar.copy(h2[t][:, halves[u][0]], h2_ps[u][t][:])
         for t in range(PACK):
             for cols, part_list in halves:
                 if t != 1:
                     nc.vector.tensor_copy(far[t][:, cols], h2[t][:].indirect(n3_t[:, part_list]))
                 else:
                     nc.scalar.activation(far[t][:, cols], h2[t][:].indirect(n3_t[:, part_list]), ACT.Copy)
-            nc.vector.tensor_tensor(st[t][:], h2_ps[t][:], far[t][:], ALU.subtract)
+            for u in range(2):
+                cols = halves[u][0]
+                nc.vector.tensor_tensor(st[t][:, cols], h2_ps[u][t][:], far[t][:, cols], ALU.subtract)
         for t in range(PACK):
             for cols, part_list in halves:
                 nc.scalar.activation(
                     sg[t][:, cols], st[t][:].indirect(n4_t[:, part_list]), ACT.Sigmoid,
                     bias=bias_c[:, t : t + 1], scale=sl_c[:, t : t + 1],
                 )
-        for t in range(PACK):
-            for u in range(2):
-                cols = halves[u][0]
-                nc.vector.tensor_tensor(y[u][:, t, :], h2_ps[t][:, cols], sg[t][:, cols], ALU.mult)
+        y = [keep.tile([P, PACK, HALF], F32, name=f"y{u}", tag=f"far{3 - u}", align_bytes=64) for u in range(2)]
+        for u in range(2):
+            cols = halves[u][0]
+            for t in range(PACK):
+                nc.vector.tensor_tensor(y[u][:, t, :], h2_ps[u][t][:], sg[t][:, cols], ALU.mult)
                 nc.sync.dma_start(out_rows[:, t, cols], y[u][:, t, :])
         for u in range(2):
-            cols = slice(HALF * u, HALF * (u + 1))
-            nc.vector.tensor_copy(y_in[u][:], y[u][:].rearrange("p t c -> p c t"))
+            cols = halves[u][0]
+            grouped = y_in[u][:].rearrange("p (c i) t -> p c t i", i=4)
+            rows = y[u][:].rearrange("p t (c i) -> p c t i", i=4)
+            if u == 0:
+                nc.scalar.copy(grouped, rows)
+            else:
+                nc.vector.tensor_copy(grouped, rows)
+        for u in range(2):
+            cols = halves[u][0]
             nc.vector.quantize_mx(y_word[u][:].bitcast(FP8X4), y_scale[u][:], y_in[u][:].rearrange("p c t -> p (c t)"))
             nc.sync.dma_start(out_words[:, cols], y_word[u][:])
             for q in range(4):

@@ -60,6 +60,9 @@ def tile_picked_pqlayknormehq_none_po_kernel(
         nc.gpsimd.memset(x_scale_tab[:].bitcast(I32), 0)
         load_scale_rows(nc.gpsimd, x_scale_tab, x_scales[0])
 
+        warm = tile("warm", 16, F32)
+        nc.gpsimd.memset(warm[:, 0:1], 1.0)
+        nc.scalar.activation(warm[:, 8:9], warm[:, 0:1], ACT.Abs_reciprocal_sqrt)
         d_scale_got = keep.tile([P, H], U8, name="d_scale_got", tag="scale_stage", align_bytes=64)
         nc.vector.tensor_copy(d_scale_got[:], d_scale_tab[:].indirect(k1_t[:]))
         w_word_raw = keep.tile([P, 2 * N], U8, name="w_word_raw", tag="early", align_bytes=64)
@@ -151,6 +154,7 @@ def tile_picked_pqlayknormehq_none_po_kernel(
             for u in range(2):
                 cols = slice(HALF * u, HALF * (u + 1))
                 nc.vector.tensor_scalar(z_rows[:, t, cols], ds[t][:, cols], gn_c[:, t : t + 1], None, ALU.mult)
+        nc.scalar.activation(warm[:, 9:10], z_rows[:, 1, 0:1], ACT.Sigmoid)
 
         h2_ps = [
             [psum.tile([P, HALF], F32, name=f"h2_ps{u}{t}", tag=f"bank{PACK * (1 - u) + t}") for t in range(PACK)]

@@ -18,7 +18,15 @@ ACT = mybir.ActivationFunctionType
 
 P = 128
 PACK = 4
+QUAD = 32
+BLOCK_P = 8
 HALF = S // 2
+RUN = 4
+
+SCALAR_SCATTERS = (0, 1)
+VECTOR_SCATTERS = (2, 3)
+SCALAR_GATHERS = 1
+VECTOR_GAINS = 3
 
 
 def tile_picked_pqlayknormehq_none_po_kernel(
@@ -29,207 +37,193 @@ def tile_picked_pqlayknormehq_none_po_kernel(
         keep = ctx.enter_context(tc.tile_pool(name="keep", bufs=1))
         psum = ctx.enter_context(tc.psum_pool(name="psum", bufs=1))
 
-        def tile(name, width, dtype):
-            return keep.tile([P, width], dtype, name=name, align_bytes=64)
+        def tile(name, shape, dtype, reuse=None):
+            return keep.tile([P, *shape], dtype, name=name, tag=reuse or name, align_bytes=64)
+
+        def tiles(name, which, width, dtype):
+            return {t: tile(f"{name}{t}", [width], dtype) for t in which}
 
         def load_list(name, src):
             lst = keep.tile([P, src.shape[1]], U16, name=name)
             nc.sync.dma_start(lst[:], src)
             return lst
 
-        def load_scale_rows(queue, plane, rows):
-            for q in range(4):
-                queue.dma_start(plane[32 * q : 32 * q + 4, :].bitcast(I32), rows[4 * q : 4 * q + 4, :].bitcast(I32))
+        def as_words(src):
+            return src[0].rearrange("p n t -> p (n t)").bitcast(I32)
 
-        d_scale_tab = keep.tile([P, G], U8, name="d_scale_tab", tag="early", align_bytes=64)
+        def deal(copy, dst, src):
+            copy(dst.rearrange("p (t m) -> p t m", t=PACK), src.rearrange("p (m t) -> p t m", t=PACK))
+
+        def gather(t, dst, window):
+            if t == SCALAR_GATHERS:
+                nc.scalar.activation(dst, window, ACT.Copy)
+            else:
+                nc.vector.tensor_copy(dst, window)
+
+        def interleave(copy, dst, rows):
+            copy(dst.rearrange("p (c i) t -> p c t i", i=RUN), rows.rearrange("p t (c i) -> p c t i", i=RUN))
+
+        def quantize(words, scales, grouped):
+            nc.vector.quantize_mx(words.bitcast(FP8X4), scales, grouped.rearrange("p c t -> p (c t)"))
+
+        every = range(PACK)
+        halves = [slice(HALF * u, HALF * (u + 1)) for u in range(2)]
+        list_halves = [slice(HALF // 16 * u, HALF // 16 * (u + 1)) for u in range(2)]
+
+        d_scale_tab = tile("d_scale_tab", [G], U8)
         nc.sync.dma_start(
-            d_scale_tab[:].bitcast(I32),
-            d_scales[0].bitcast(I32).unsqueeze(1).to_broadcast([16, 8, G // 4]),
+            d_scale_tab[:].bitcast(I32), d_scales[0].bitcast(I32).unsqueeze(1).to_broadcast([16, BLOCK_P, G // 4])
         )
-        k1_t = load_list("k1_t", k1)
-        offs_t = load_list("offs_t", offs)
-        n2_t = load_list("n2_t", n2)
-        d_word_tab = keep.tile([P, G], I32, name="d_word_tab", tag="d_words", align_bytes=64)
-        nc.sync.dma_start(d_word_tab[:], d_words[0].rearrange("p n t -> p (n t)").bitcast(I32))
-        n1_t = load_list("n1_t", n1)
-        n3_t = load_list("n3_t", n3)
-        n4_t = load_list("n4_t", n4)
-        x_word_tab = keep.tile([P, T], I32, name="x_word_tab", tag="x_words", align_bytes=64)
-        nc.sync.dma_start(x_word_tab[:], x_words[0].rearrange("p n t -> p (n t)").bitcast(I32))
-        x_scale_tab = tile("x_scale_tab", T, U8)
-        nc.gpsimd.memset(x_scale_tab[:].bitcast(I32), 0)
-        load_scale_rows(nc.gpsimd, x_scale_tab, x_scales[0])
+        k1_list = load_list("k1_list", k1)
+        d_word_tab = tile("d_word_tab", [G], I32)
+        nc.sync.dma_start(d_word_tab[:], as_words(d_words))
+        x_scale_tab = tile("x_scale_tab", [T], U8)
+        for q in range(4):
+            nc.sync.dma_start(
+                x_scale_tab[QUAD * q : QUAD * (q + 1), :].bitcast(I32),
+                x_scales[0][4 * q : 4 * q + 4, :].bitcast(I32).unsqueeze(0).to_broadcast([QUAD // 4, 4, T // 4]),
+            )
+        offs_list = load_list("offs_list", offs)
+        x_word_tab = tile("x_word_tab", [T], I32)
+        nc.sync.dma_start(x_word_tab[:], as_words(x_words))
+        n2_list = load_list("n2_list", n2)
+        n1_list = load_list("n1_list", n1)
+        n3_list = load_list("n3_list", n3)
+        n4_list = load_list("n4_list", n4)
+        w_scale_raw = tile("w_scale_raw", [N], U8)
+        nc.gpsimd.memset(w_scale_raw[:].bitcast(I32), 0)
+        for q in range(4):
+            nc.gpsimd.dma_start(
+                w_scale_raw[QUAD * q : QUAD * q + 4, :].bitcast(I32), w1_scales[0][4 * q : 4 * q + 4, :].bitcast(I32)
+            )
 
-        warm = tile("warm", 16, F32)
+        warm = tile("warm", [16], F32)
         nc.gpsimd.memset(warm[:, 0:1], 1.0)
         nc.scalar.activation(warm[:, 8:9], warm[:, 0:1], ACT.Abs_reciprocal_sqrt)
-        d_scale_got = keep.tile([P, H], U8, name="d_scale_got", tag="scale_stage", align_bytes=64)
-        nc.vector.tensor_copy(d_scale_got[:], d_scale_tab[:].indirect(k1_t[:]))
-        w_word_raw = keep.tile([P, 2 * N], U8, name="w_word_raw", tag="early", align_bytes=64)
+
+        d_scale_got = tile("d_scale_got", [H], U8)
+        nc.vector.tensor_copy(d_scale_got[:], d_scale_tab[:].indirect(k1_list[:]))
+        w_word_raw = tile("w_word_raw", [2 * N], U8, reuse="d_scale_tab")
         nc.gpsimd.dma_start(w_word_raw[:].bitcast(I32), w1_words[0].bitcast(I32))
-        d_scale = tile("d_scale", H, U8)
-        nc.vector.tensor_copy(
-            d_scale[:].rearrange("p (t m) -> p t m", t=PACK), d_scale_got[:].rearrange("p (m t) -> p t m", t=PACK)
-        )
+        d_scale = tile("d_scale", [H], U8)
+        deal(nc.vector.tensor_copy, d_scale[:], d_scale_got[:])
         for r in range(1, 4):
-            nc.scalar.dma_start(d_scale[r:P:32, :].bitcast(I32), d_scale[8 * r : P : 32, :].bitcast(I32))
-        w_scale_raw = keep.tile([P, N], U8, name="w_scale_raw", tag="scale_stage", align_bytes=64)
-        nc.vector.memset(w_scale_raw[:].bitcast(I32), 0)
-        load_scale_rows(nc.scalar, w_scale_raw, w1_scales[0])
-        d_word_got = keep.tile([P, H], I32, name="d_word_got", tag="word_stage", align_bytes=64)
-        nc.vector.tensor_copy(d_word_got[:].bitcast(U32), d_word_tab[:].bitcast(U32).indirect(k1_t[:]))
-        d_word = tile("d_word", H, I32)
-        nc.vector.tensor_copy(
-            d_word[:].rearrange("p (t m) -> p t m", t=PACK), d_word_got[:].rearrange("p (m t) -> p t m", t=PACK)
-        )
-        per_row = keep.tile([P, 3, 8], F32, name="per_row", tag="word_stage", align_bytes=64)
+            nc.scalar.dma_start(d_scale[r:P:QUAD, :].bitcast(I32), d_scale[BLOCK_P * r : P : QUAD, :].bitcast(I32))
+        d_word_got = tile("d_word_got", [H], I32)
+        nc.vector.tensor_copy(d_word_got[:].bitcast(U32), d_word_tab[:].bitcast(U32).indirect(k1_list[:]))
+        d_word = tile("d_word", [H], I32)
+        deal(nc.vector.tensor_copy, d_word[:], d_word_got[:])
+        per_row = tile("per_row", [3, 8], F32, reuse="d_word_got")
         for slot, src in enumerate((gn, sl, th)):
-            nc.gpsimd.dma_start(per_row[:, slot, 0:PACK], src.rearrange("(p t) o -> p (t o)", t=PACK))
-        gn_c, sl_c, th_c = (per_row[:, slot, :] for slot in range(3))
-        x_scale = keep.tile([P, S], U8, name="x_scale", tag="d_words", align_bytes=64)
-        nc.vector.tensor_copy(x_scale[:], x_scale_tab[:].indirect(offs_t[:]))
-        x_word = tile("x_word", S, I32)
-        nc.vector.tensor_copy(x_word[:].bitcast(U32), x_word_tab[:].bitcast(U32).indirect(offs_t[:]))
+            nc.sync.dma_start(per_row[:, slot, 0:PACK], src.rearrange("(p t) o -> p (t o)", t=PACK))
+        gain, slope, threshold = (per_row[:, slot, 0:PACK] for slot in range(3))
+        x_scale = tile("x_scale", [S], U8)
+        nc.vector.tensor_copy(x_scale[:], x_scale_tab[:].indirect(offs_list[:]))
+        x_word = tile("x_word", [S], I32)
+        nc.vector.tensor_copy(x_word[:].bitcast(U32), x_word_tab[:].bitcast(U32).indirect(offs_list[:]))
 
-        w_word = tile("w_word", 2 * N, U8)
-        nc.scalar.copy(
-            w_word[:].bitcast(U16).rearrange("p (t m) -> p t m", t=PACK),
-            w_word_raw[:].bitcast(U16).rearrange("p (m t) -> p t m", t=PACK),
-        )
-        w_scale = keep.tile([P, N], U8, name="w_scale", tag="x_words", align_bytes=64)
-        nc.vector.tensor_copy(
-            w_scale[:].rearrange("p (t m) -> p t m", t=PACK), w_scale_raw[:].rearrange("p (m t) -> p t m", t=PACK)
-        )
-        bias_c = tile("bias_c", PACK, F32)
-        sl_th = tile("sl_th", PACK, F32)
-        nc.gpsimd.tensor_tensor(sl_th[:], sl_c[:, 0:PACK], th_c[:, 0:PACK], ALU.mult)
-        nc.gpsimd.tensor_scalar(bias_c[:], sl_th[:], -1.0, 0.0, ALU.mult, ALU.add)
+        w_word = tile("w_word", [2 * N], U8)
+        deal(nc.scalar.copy, w_word[:].bitcast(U16), w_word_raw[:].bitcast(U16))
+        w_scale = tile("w_scale", [N], U8, reuse="x_word_tab")
+        deal(nc.vector.tensor_copy, w_scale[:], w_scale_raw[:])
+        slope_threshold = tile("slope_threshold", [PACK], F32)
+        nc.gpsimd.tensor_tensor(slope_threshold[:], slope, threshold, ALU.mult)
+        bias = tile("bias", [PACK], F32)
+        nc.gpsimd.tensor_scalar(bias[:], slope_threshold[:], -1.0, 0.0, ALU.mult, ALU.add)
 
-        h_ps = [psum.tile([P, S], F32, name=f"h_ps{t}", tag=f"bank{t}") for t in range(PACK)]
-        for t in range(PACK):
+        h_ps = [psum.tile([P, S], F32, name=f"h_ps{t}", tag=f"bank{t}") for t in every]
+        for t in every:
             cols = slice(P * t, P * (t + 1))
             nc.tensor.matmul_mx(
                 h_ps[t][:], lhsT=d_word[:, cols].bitcast(FP8X4), lhsT_scale=d_scale[:, cols],
                 rhs=x_word[:].bitcast(FP8X4), rhs_scale=x_scale[:], start=True, stop=True,
             )
 
-        def work(name, tag=None):
-            return keep.tile([P, W], F32, name=name, tag=tag or name, align_bytes=64)
-
-        ds = [tile(f"ds{t}", S, F32) for t in range(PACK)]
-        pa = [work(f"pa{t}") for t in range(PACK)]
-        mag = [keep.tile([P, W], F32, name=f"mag{t}", tag=f"mag{t}", align_bytes=64) for t in range(PACK)]
-        root = [work(f"root{t}") for t in range(PACK)]
-        inv = [work(f"inv{t}") for t in range(2)]
-        old = [work(f"old{t}") for t in range(PACK)]
-        z_rows = keep.tile([P, PACK, S], BF16, name="z_rows", align_bytes=64)
-
-        for t in range(PACK):
+        ds = tiles("ds", every, S, F32)
+        pa, old, size, root = (tiles(name, every, W, F32) for name in ("pa", "old", "size", "root"))
+        inverse = tiles("inverse", SCALAR_SCATTERS, W, F32)
+        z_rows = tile("z_rows", [PACK, S], BF16)
+        for t in every:
             nc.scalar.activation(ds[t][:], h_ps[t][:], ACT.Copy, scale=0.0625)
-        for t in range(PACK):
-            nc.vector.tensor_copy(pa[t][:], ds[t][:].indirect(n2_t[:]))
-        for t in range(PACK):
-            if t == 1:
-                nc.scalar.activation(old[t][:], ds[t][:].indirect(n1_t[:]), ACT.Copy)
-            else:
-                nc.vector.tensor_copy(old[t][:], ds[t][:].indirect(n1_t[:]))
-        for t in range(PACK):
-            nc.scalar.activation(mag[t][:], pa[t][:], ACT.Abs)
-            nc.scalar.activation(root[t][:], mag[t][:], ACT.Abs_reciprocal_sqrt, bias=0.5)
-            if t < 2:
-                nc.scalar.activation(inv[t][:], root[t][:], ACT.Square)
-        ra = keep.tile([P, 2, W], F32, name="ra", tag="mag2", align_bytes=64)
-        for t in range(2):
-            nc.vector.tensor_tensor(ra[:, t, :], old[t][:], inv[t][:], ALU.mult)
-        part = {2: work("part2", "old1"), 3: work("part3", "inv1")}
-        for t in range(2, PACK):
-            nc.vector.tensor_tensor(part[t][:], old[t][:], root[t][:], ALU.mult)
-        for t in range(2):
-            nc.scalar.activation(ds[t][:].indirect(n1_t[:]), ra[:, t, :], ACT.Copy)
-        for t in range(2, PACK):
-            nc.vector.tensor_tensor(ds[t][:].indirect(n1_t[:]), part[t][:], root[t][:], ALU.mult)
-        for t in range(2):
-            nc.scalar.activation(z_rows[:, t, :], ds[t][:], ACT.Copy, scale=gn_c[:, t : t + 1])
-        for t in range(2, PACK):
-            for u in range(2):
-                cols = slice(HALF * u, HALF * (u + 1))
-                nc.vector.tensor_scalar(z_rows[:, t, cols], ds[t][:, cols], gn_c[:, t : t + 1], None, ALU.mult)
-        nc.scalar.activation(warm[:, 9:10], z_rows[:, 1, 0:1], ACT.Sigmoid)
+        for t in every:
+            nc.vector.tensor_copy(pa[t][:], ds[t][:].indirect(n2_list[:]))
+        for t in every:
+            gather(t, old[t][:], ds[t][:].indirect(n1_list[:]))
+        for t in every:
+            nc.scalar.activation(size[t][:], pa[t][:], ACT.Abs)
+            nc.scalar.activation(root[t][:], size[t][:], ACT.Abs_reciprocal_sqrt, bias=0.5)
+            if t in SCALAR_SCATTERS:
+                nc.scalar.activation(inverse[t][:], root[t][:], ACT.Square)
+        ra = tile("ra", [len(SCALAR_SCATTERS), W], F32, reuse="size2")
+        for t in SCALAR_SCATTERS:
+            nc.vector.tensor_tensor(ra[:, t, :], old[t][:], inverse[t][:], ALU.mult)
+        old_root = {t: tile(f"old_root{t}", [W], F32, reuse=name) for t, name in zip(VECTOR_SCATTERS, ("old1", "inverse1"))}
+        for t in VECTOR_SCATTERS:
+            nc.vector.tensor_tensor(old_root[t][:], old[t][:], root[t][:], ALU.mult)
+        for t in SCALAR_SCATTERS:
+            nc.scalar.activation(ds[t][:].indirect(n1_list[:]), ra[:, t, :], ACT.Copy)
+        for t in VECTOR_SCATTERS:
+            nc.vector.tensor_tensor(ds[t][:].indirect(n1_list[:]), old_root[t][:], root[t][:], ALU.mult)
+        for t in range(VECTOR_GAINS):
+            nc.scalar.activation(z_rows[:, t, :], ds[t][:], ACT.Copy, scale=gain[:, t : t + 1])
+        for cols in halves:
+            nc.vector.tensor_scalar(
+                z_rows[:, VECTOR_GAINS, cols], ds[VECTOR_GAINS][:, cols], gain[:, VECTOR_GAINS : VECTOR_GAINS + 1], None, ALU.mult
+            )
+        nc.scalar.activation(warm[:, 9:10], z_rows[:, VECTOR_GAINS - 1, 0:1], ACT.Sigmoid)
 
         h2_ps = [
-            [psum.tile([P, HALF], F32, name=f"h2_ps{u}{t}", tag=f"bank{PACK * (1 - u) + t}") for t in range(PACK)]
+            [psum.tile([P, HALF], F32, name=f"h2_ps{u}{t}", tag=f"bank{PACK * (1 - u) + t}") for t in every]
             for u in range(2)
         ]
-        z_in = [keep.tile([P, HALF, PACK], BF16, name=f"z_in{u}", align_bytes=64) for u in range(2)]
-        z_word = [tile(f"z_word{u}", HALF, U32) for u in range(2)]
-        z_scale = [tile(f"z_scale{u}", HALF, U8) for u in range(2)]
+        z_grouped = [tile(f"z_grouped{u}", [HALF, PACK], BF16) for u in range(2)]
+        z_word = tiles("z_word", range(2), HALF, U32)
+        z_scale = tiles("z_scale", range(2), HALF, U8)
         for u in range(2):
             nc.gpsimd.memset(z_scale[u][:].bitcast(I32), 0)
         for u in range(2):
-            cols = slice(HALF * u, HALF * (u + 1))
-            nc.vector.tensor_copy(
-                z_in[u][:].rearrange("p (c i) t -> p c t i", i=4), z_rows[:, :, cols].rearrange("p t (c i) -> p c t i", i=4)
-            )
+            interleave(nc.vector.tensor_copy, z_grouped[u][:], z_rows[:, :, halves[u]])
         for u in range(2):
-            nc.vector.quantize_mx(z_word[u][:].bitcast(FP8X4), z_scale[u][:], z_in[u][:].rearrange("p c t -> p (c t)"))
+            quantize(z_word[u][:], z_scale[u][:], z_grouped[u][:])
         for u in range(2):
-            cols = slice(HALF * u, HALF * (u + 1))
-            for t in range(PACK):
+            for t in every:
                 nc.tensor.matmul_mx(
                     h2_ps[u][t][:], lhsT=w_word[:, 2 * P * t : 2 * P * (t + 1)].bitcast(FP4X4),
                     lhsT_scale=w_scale[:, P * t : P * (t + 1)],
                     rhs=z_word[u][:].bitcast(FP8X4), rhs_scale=z_scale[u][:], start=True, stop=True,
                 )
 
-        h2 = [tile(f"h2_{t}", S, F32) for t in range(PACK)]
-        far = [keep.tile([P, S], F32, name=f"far{t}", tag=f"far{t}", align_bytes=64) for t in range(PACK)]
-        st = [tile(f"st{t}", S, F32) for t in range(PACK)]
-        sg = [tile(f"sg{t}", S, F32) for t in range(PACK)]
-        y_in = [keep.tile([P, HALF, PACK], BF16, name=f"y_in{u}", align_bytes=64) for u in range(2)]
-        y_word = [tile(f"y_word{u}", HALF, I32) for u in range(2)]
-        y_scale = [tile(f"y_scale{u}", HALF, U8) for u in range(2)]
-        out_rows = out_0.rearrange("(p t) c -> p t c", t=PACK)
-        out_words = out_1[0].rearrange("p n t -> p (n t)").bitcast(I32)
-        LC = HALF // 16
-        halves = [(slice(HALF * u, HALF * (u + 1)), slice(LC * u, LC * (u + 1))) for u in range(2)]
+        h2, h2_n3, st, sg = (tiles(name, every, S, F32) for name in ("h2_", "h2_n3_", "st", "sg"))
         for u in range(2):
-            for t in range(PACK):
-                nc.scalar.copy(h2[t][:, halves[u][0]], h2_ps[u][t][:])
-        for t in range(PACK):
-            for cols, part_list in halves:
-                if t != 1:
-                    nc.vector.tensor_copy(far[t][:, cols], h2[t][:].indirect(n3_t[:, part_list]))
-                else:
-                    nc.scalar.activation(far[t][:, cols], h2[t][:].indirect(n3_t[:, part_list]), ACT.Copy)
+            for t in every:
+                nc.scalar.copy(h2[t][:, halves[u]], h2_ps[u][t][:])
+        for t in every:
             for u in range(2):
-                cols = halves[u][0]
-                nc.vector.tensor_tensor(st[t][:, cols], h2_ps[u][t][:], far[t][:, cols], ALU.subtract)
-        for t in range(PACK):
-            for cols, part_list in halves:
+                gather(t, h2_n3[t][:, halves[u]], h2[t][:].indirect(n3_list[:, list_halves[u]]))
+            for u in range(2):
+                nc.vector.tensor_tensor(st[t][:, halves[u]], h2_ps[u][t][:], h2_n3[t][:, halves[u]], ALU.subtract)
+        for t in every:
+            for u in range(2):
                 nc.scalar.activation(
-                    sg[t][:, cols], st[t][:].indirect(n4_t[:, part_list]), ACT.Sigmoid,
-                    bias=bias_c[:, t : t + 1], scale=sl_c[:, t : t + 1],
+                    sg[t][:, halves[u]], st[t][:].indirect(n4_list[:, list_halves[u]]), ACT.Sigmoid,
+                    bias=bias[:, t : t + 1], scale=slope[:, t : t + 1],
                 )
-        y = [keep.tile([P, PACK, HALF], F32, name=f"y{u}", tag=f"far{3 - u}", align_bytes=64) for u in range(2)]
+        y = [tile(f"y{u}", [PACK, HALF], F32, reuse=f"h2_n3_{PACK - 1 - u}") for u in range(2)]
+        out_rows = out_0.rearrange("(p t) c -> p t c", t=PACK)
         for u in range(2):
-            cols = halves[u][0]
-            for t in range(PACK):
-                nc.vector.tensor_tensor(y[u][:, t, :], h2_ps[u][t][:], sg[t][:, cols], ALU.mult)
-                nc.sync.dma_start(out_rows[:, t, cols], y[u][:, t, :])
+            for t in every:
+                nc.vector.tensor_tensor(y[u][:, t, :], h2_ps[u][t][:], sg[t][:, halves[u]], ALU.mult)
+                if t % 2 == 1:
+                    nc.sync.dma_start(out_rows[:, t - 1 : t + 1, halves[u]], y[u][:, t - 1 : t + 1, :])
+
+        y_grouped = [tile(f"y_grouped{u}", [HALF, PACK], BF16) for u in range(2)]
+        y_word = tiles("y_word", range(2), HALF, I32)
+        y_scale = tile("y_scale", [S], U8)
+        for u, copy in enumerate((nc.scalar.copy, nc.vector.tensor_copy)):
+            interleave(copy, y_grouped[u][:], y[u][:])
         for u in range(2):
-            cols = halves[u][0]
-            grouped = y_in[u][:].rearrange("p (c i) t -> p c t i", i=4)
-            rows = y[u][:].rearrange("p t (c i) -> p c t i", i=4)
-            if u == 0:
-                nc.scalar.copy(grouped, rows)
-            else:
-                nc.vector.tensor_copy(grouped, rows)
-        for u in range(2):
-            cols = halves[u][0]
-            nc.vector.quantize_mx(y_word[u][:].bitcast(FP8X4), y_scale[u][:], y_in[u][:].rearrange("p c t -> p (c t)"))
-            nc.sync.dma_start(out_words[:, cols], y_word[u][:])
-            for q in range(4):
-                queue = nc.sync if q % 2 == 0 else nc.scalar
-                queue.dma_start(
-                    out_2[0][4 * q : 4 * q + 4, cols].bitcast(I32), y_scale[u][32 * q : 32 * q + 4, :].bitcast(I32)
-                )
+            quantize(y_word[u][:], y_scale[:, halves[u]], y_grouped[u][:])
+            nc.sync.dma_start(as_words(out_1)[:, halves[u]], y_word[u][:])
+        for q in range(4):
+            queue = nc.scalar if q < 2 else nc.sync
+            queue.dma_start(out_2[0][4 * q : 4 * q + 4, :].bitcast(I32), y_scale[QUAD * q : QUAD * q + 4, :].bitcast(I32))

from contextlib import ExitStack

import concourse.mybir as mybir

K, T, S, N, G, H, W = 512, 2048, 512, 512, 2048, 512, 384
FLOPS = 2 * K * H * S + 2 * H * N * S

F32 = mybir.dt.float32
BF16 = mybir.dt.bfloat16
I32 = mybir.dt.int32
U32 = mybir.dt.uint32
U16 = mybir.dt.uint16
U8 = mybir.dt.uint8
FP8X4 = mybir.dt.float8_e4m3fn_x4
FP4X4 = mybir.dt.float4_e2m1fn_x4
ALU = mybir.AluOpType
ACT = mybir.ActivationFunctionType

P = 128
PACK = 4
QUAD = 32
BLOCK_P = 8
HALF = S // 2
RUN = 4

SCALAR_SCATTERS = (0, 1)
VECTOR_SCATTERS = (2, 3)
SCALAR_GATHERS = 1
VECTOR_GAINS = 3


def tile_picked_pqlayknormehq_none_po_kernel(
    tc, x_words, x_scales, d_words, d_scales, gn, w1_words, w1_scales, sl, th, offs, k1, n1, n2, n3, n4, out_0, out_1, out_2
):
    nc = tc.nc
    with ExitStack() as ctx:
        keep = ctx.enter_context(tc.tile_pool(name="keep", bufs=1))
        psum = ctx.enter_context(tc.psum_pool(name="psum", bufs=1))

        def tile(name, shape, dtype, reuse=None):
            return keep.tile([P, *shape], dtype, name=name, tag=reuse or name, align_bytes=64)

        def tiles(name, which, width, dtype):
            return {t: tile(f"{name}{t}", [width], dtype) for t in which}

        def load_list(name, src):
            lst = keep.tile([P, src.shape[1]], U16, name=name)
            nc.sync.dma_start(lst[:], src)
            return lst

        def as_words(src):
            return src[0].rearrange("p n t -> p (n t)").bitcast(I32)

        def deal(copy, dst, src):
            copy(dst.rearrange("p (t m) -> p t m", t=PACK), src.rearrange("p (m t) -> p t m", t=PACK))

        def gather(t, dst, window):
            if t == SCALAR_GATHERS:
                nc.scalar.activation(dst, window, ACT.Copy)
            else:
                nc.vector.tensor_copy(dst, window)

        def interleave(copy, dst, rows):
            copy(dst.rearrange("p (c i) t -> p c t i", i=RUN), rows.rearrange("p t (c i) -> p c t i", i=RUN))

        def quantize(words, scales, grouped):
            nc.vector.quantize_mx(words.bitcast(FP8X4), scales, grouped.rearrange("p c t -> p (c t)"))

        every = range(PACK)
        halves = [slice(HALF * u, HALF * (u + 1)) for u in range(2)]
        list_halves = [slice(HALF // 16 * u, HALF // 16 * (u + 1)) for u in range(2)]

        d_scale_tab = tile("d_scale_tab", [G], U8)
        nc.sync.dma_start(
            d_scale_tab[:].bitcast(I32), d_scales[0].bitcast(I32).unsqueeze(1).to_broadcast([16, BLOCK_P, G // 4])
        )
        k1_list = load_list("k1_list", k1)
        d_word_tab = tile("d_word_tab", [G], I32)
        nc.sync.dma_start(d_word_tab[:], as_words(d_words))
        x_scale_tab = tile("x_scale_tab", [T], U8)
        for q in range(4):
            nc.sync.dma_start(
                x_scale_tab[QUAD * q : QUAD * (q + 1), :].bitcast(I32),
                x_scales[0][4 * q : 4 * q + 4, :].bitcast(I32).unsqueeze(0).to_broadcast([QUAD // 4, 4, T // 4]),
            )
        offs_list = load_list("offs_list", offs)
        x_word_tab = tile("x_word_tab", [T], I32)
        nc.sync.dma_start(x_word_tab[:], as_words(x_words))
        n2_list = load_list("n2_list", n2)
        n1_list = load_list("n1_list", n1)
        n3_list = load_list("n3_list", n3)
        n4_list = load_list("n4_list", n4)
        w_scale_raw = tile("w_scale_raw", [N], U8)
        nc.gpsimd.memset(w_scale_raw[:].bitcast(I32), 0)
        for q in range(4):
            nc.gpsimd.dma_start(
                w_scale_raw[QUAD * q : QUAD * q + 4, :].bitcast(I32), w1_scales[0][4 * q : 4 * q + 4, :].bitcast(I32)
            )

        warm = tile("warm", [16], F32)
        nc.gpsimd.memset(warm[:, 0:1], 1.0)
        nc.scalar.activation(warm[:, 8:9], warm[:, 0:1], ACT.Abs_reciprocal_sqrt)

        d_scale_got = tile("d_scale_got", [H], U8)
        nc.vector.tensor_copy(d_scale_got[:], d_scale_tab[:].indirect(k1_list[:]))
        w_word_raw = tile("w_word_raw", [2 * N], U8, reuse="d_scale_tab")
        nc.gpsimd.dma_start(w_word_raw[:].bitcast(I32), w1_words[0].bitcast(I32))
        d_scale = tile("d_scale", [H], U8)
        deal(nc.vector.tensor_copy, d_scale[:], d_scale_got[:])
        for r in range(1, 4):
            nc.scalar.dma_start(d_scale[r:P:QUAD, :].bitcast(I32), d_scale[BLOCK_P * r : P : QUAD, :].bitcast(I32))
        d_word_got = tile("d_word_got", [H], I32)
        nc.vector.tensor_copy(d_word_got[:].bitcast(U32), d_word_tab[:].bitcast(U32).indirect(k1_list[:]))
        d_word = tile("d_word", [H], I32)
        deal(nc.vector.tensor_copy, d_word[:], d_word_got[:])
        per_row = tile("per_row", [3, 8], F32, reuse="d_word_got")
        for slot, src in enumerate((gn, sl, th)):
            nc.sync.dma_start(per_row[:, slot, 0:PACK], src.rearrange("(p t) o -> p (t o)", t=PACK))
        gain, slope, threshold = (per_row[:, slot, 0:PACK] for slot in range(3))
        x_scale = tile("x_scale", [S], U8)
        nc.vector.tensor_copy(x_scale[:], x_scale_tab[:].indirect(offs_list[:]))
        x_word = tile("x_word", [S], I32)
        nc.vector.tensor_copy(x_word[:].bitcast(U32), x_word_tab[:].bitcast(U32).indirect(offs_list[:]))

        w_word = tile("w_word", [2 * N], U8)
        deal(nc.scalar.copy, w_word[:].bitcast(U16), w_word_raw[:].bitcast(U16))
        w_scale = tile("w_scale", [N], U8, reuse="x_word_tab")
        deal(nc.vector.tensor_copy, w_scale[:], w_scale_raw[:])
        slope_threshold = tile("slope_threshold", [PACK], F32)
        nc.gpsimd.tensor_tensor(slope_threshold[:], slope, threshold, ALU.mult)
        bias = tile("bias", [PACK], F32)
        nc.gpsimd.tensor_scalar(bias[:], slope_threshold[:], -1.0, 0.0, ALU.mult, ALU.add)

        h_ps = [psum.tile([P, S], F32, name=f"h_ps{t}", tag=f"bank{t}") for t in every]
        for t in every:
            cols = slice(P * t, P * (t + 1))
            nc.tensor.matmul_mx(
                h_ps[t][:], lhsT=d_word[:, cols].bitcast(FP8X4), lhsT_scale=d_scale[:, cols],
                rhs=x_word[:].bitcast(FP8X4), rhs_scale=x_scale[:], start=True, stop=True,
            )

        ds = tiles("ds", every, S, F32)
        pa, old, size, root = (tiles(name, every, W, F32) for name in ("pa", "old", "size", "root"))
        inverse = tiles("inverse", SCALAR_SCATTERS, W, F32)
        z_rows = tile("z_rows", [PACK, S], BF16)
        for t in every:
            nc.scalar.activation(ds[t][:], h_ps[t][:], ACT.Copy, scale=0.0625)
        for t in every:
            nc.vector.tensor_copy(pa[t][:], ds[t][:].indirect(n2_list[:]))
        for t in every:
            gather(t, old[t][:], ds[t][:].indirect(n1_list[:]))
        for t in every:
            nc.scalar.activation(size[t][:], pa[t][:], ACT.Abs)
            nc.scalar.activation(root[t][:], size[t][:], ACT.Abs_reciprocal_sqrt, bias=0.5)
            if t in SCALAR_SCATTERS:
                nc.scalar.activation(inverse[t][:], root[t][:], ACT.Square)
        ra = tile("ra", [len(SCALAR_SCATTERS), W], F32, reuse="size2")
        for t in SCALAR_SCATTERS:
            nc.vector.tensor_tensor(ra[:, t, :], old[t][:], inverse[t][:], ALU.mult)
        old_root = {t: tile(f"old_root{t}", [W], F32, reuse=name) for t, name in zip(VECTOR_SCATTERS, ("old1", "inverse1"))}
        for t in VECTOR_SCATTERS:
            nc.vector.tensor_tensor(old_root[t][:], old[t][:], root[t][:], ALU.mult)
        for t in SCALAR_SCATTERS:
            nc.scalar.activation(ds[t][:].indirect(n1_list[:]), ra[:, t, :], ACT.Copy)
        for t in VECTOR_SCATTERS:
            nc.vector.tensor_tensor(ds[t][:].indirect(n1_list[:]), old_root[t][:], root[t][:], ALU.mult)
        for t in range(VECTOR_GAINS):
            nc.scalar.activation(z_rows[:, t, :], ds[t][:], ACT.Copy, scale=gain[:, t : t + 1])
        for cols in halves:
            nc.vector.tensor_scalar(
                z_rows[:, VECTOR_GAINS, cols], ds[VECTOR_GAINS][:, cols], gain[:, VECTOR_GAINS : VECTOR_GAINS + 1], None, ALU.mult
            )
        nc.scalar.activation(warm[:, 9:10], z_rows[:, VECTOR_GAINS - 1, 0:1], ACT.Sigmoid)

        h2_ps = [
            [psum.tile([P, HALF], F32, name=f"h2_ps{u}{t}", tag=f"bank{PACK * (1 - u) + t}") for t in every]
            for u in range(2)
        ]
        z_grouped = [tile(f"z_grouped{u}", [HALF, PACK], BF16) for u in range(2)]
        z_word = tiles("z_word", range(2), HALF, U32)
        z_scale = tiles("z_scale", range(2), HALF, U8)
        for u in range(2):
            nc.gpsimd.memset(z_scale[u][:].bitcast(I32), 0)
        for u in range(2):
            interleave(nc.vector.tensor_copy, z_grouped[u][:], z_rows[:, :, halves[u]])
        for u in range(2):
            quantize(z_word[u][:], z_scale[u][:], z_grouped[u][:])
        for u in range(2):
            for t in every:
                nc.tensor.matmul_mx(
                    h2_ps[u][t][:], lhsT=w_word[:, 2 * P * t : 2 * P * (t + 1)].bitcast(FP4X4),
                    lhsT_scale=w_scale[:, P * t : P * (t + 1)],
                    rhs=z_word[u][:].bitcast(FP8X4), rhs_scale=z_scale[u][:], start=True, stop=True,
                )

        h2, h2_n3, st, sg = (tiles(name, every, S, F32) for name in ("h2_", "h2_n3_", "st", "sg"))
        for u in range(2):
            for t in every:
                nc.scalar.copy(h2[t][:, halves[u]], h2_ps[u][t][:])
        for t in every:
            for u in range(2):
                gather(t, h2_n3[t][:, halves[u]], h2[t][:].indirect(n3_list[:, list_halves[u]]))
            for u in range(2):
                nc.vector.tensor_tensor(st[t][:, halves[u]], h2_ps[u][t][:], h2_n3[t][:, halves[u]], ALU.subtract)
        for t in every:
            for u in range(2):
                nc.scalar.activation(
                    sg[t][:, halves[u]], st[t][:].indirect(n4_list[:, list_halves[u]]), ACT.Sigmoid,
                    bias=bias[:, t : t + 1], scale=slope[:, t : t + 1],
                )
        y = [tile(f"y{u}", [PACK, HALF], F32, reuse=f"h2_n3_{PACK - 1 - u}") for u in range(2)]
        out_rows = out_0.rearrange("(p t) c -> p t c", t=PACK)
        for u in range(2):
            for t in every:
                nc.vector.tensor_tensor(y[u][:, t, :], h2_ps[u][t][:], sg[t][:, halves[u]], ALU.mult)
                if t % 2 == 1:
                    nc.sync.dma_start(out_rows[:, t - 1 : t + 1, halves[u]], y[u][:, t - 1 : t + 1, :])

        y_grouped = [tile(f"y_grouped{u}", [HALF, PACK], BF16) for u in range(2)]
        y_word = tiles("y_word", range(2), HALF, I32)
        y_scale = tile("y_scale", [S], U8)
        for u, copy in enumerate((nc.scalar.copy, nc.vector.tensor_copy)):
            interleave(copy, y_grouped[u][:], y[u][:])
        for u in range(2):
            quantize(y_word[u][:], y_scale[:, halves[u]], y_grouped[u][:])
            nc.sync.dma_start(as_words(out_1)[:, halves[u]], y_word[u][:])
        for q in range(4):
            queue = nc.scalar if q < 2 else nc.sync
            queue.dma_start(out_2[0][4 * q : 4 * q + 4, :].bitcast(I32), y_scale[QUAD * q : QUAD * q + 4, :].bitcast(I32))
